import numpy as np
import ml_dtypes


def mxq(x, axis, fmt="e4m3"):
    dtype, down = {"e4m3": (ml_dtypes.float8_e4m3fn, 7), "e5m2": (ml_dtypes.float8_e5m2, 14)}[fmt]
    v = np.moveaxis(np.asarray(x, np.float32).astype(ml_dtypes.bfloat16).astype(np.float64), axis, -1)
    blocks = v.reshape(v.shape[:-1] + (-1, 32))
    amax = np.abs(blocks).max(-1, keepdims=True)
    byte = np.maximum(np.where(amax > 0, np.frexp(amax)[1] - 1 + 127, 0) - down, 1)
    scale = np.exp2(byte - 127.0)
    codes = (blocks / scale).astype(np.float32).astype(dtype).astype(np.float64)
    return np.moveaxis((codes * scale).reshape(v.shape), -1, axis)


WIDE = False


def mx_kscale(k):
    if not WIDE:
        return np.ones(k)
    levels = np.array([10, -10, 5, -5, 0])
    if k % 512:
        return np.exp2(np.random.permutation(np.resize(levels, k // 32))).repeat(32)
    a = np.empty((k // 512, 16))
    for p in range(k // 512):
        a[p, :8] = np.random.permutation(np.resize(levels, 8))
        for g in range(8):
            far = levels[np.abs(levels - a[p, g]) >= 10]
            a[p, g + 8] = far[np.random.randint(len(far))]
    return np.exp2(a.ravel()).repeat(32)


def f64(x):
    return np.asarray(x).astype(np.float64)


def striped(idx):
    return np.tile(idx.reshape(-1, 16).T, (8, 1)).astype(np.uint16)


def unstriped(offs):
    return offs[:16].T.reshape(-1).astype(np.int64)


def striped8(idx):
    return np.concatenate([x.reshape(-1, 16).T for x in idx]).astype(np.uint16)


def runs(offs, k):
    lists = np.stack([offs[16 * r : 16 * r + 16].T.reshape(-1) for r in range(8)]).astype(np.int64)
    return lists[np.arange(k) % 512 // 64]


def pack_weight(w):
    k, n = w.shape
    w = f64(np.asarray(w, np.float32).astype(ml_dtypes.bfloat16)).reshape(k // 32, 32, n)
    amax = np.abs(w).max(1)
    byte = np.clip(np.where(amax > 0, np.frexp(amax)[1] - 1 + 127 - 7, 1), 1, 254)
    scaled = (w * np.exp2(127.0 - byte)[:, None, :]).reshape(k, n).astype(np.float32)
    words = np.ascontiguousarray(scaled.reshape(k // 512, 128, 4, n).transpose(0, 1, 3, 2)).astype(ml_dtypes.float8_e4m3fn).view(np.uint8)
    return words, np.ascontiguousarray(byte.astype(np.uint8).reshape(k // 512, 16, n))


def unpack_weight(words, scales):
    g, p, n, _ = words.shape
    vals = np.ascontiguousarray(words).view(ml_dtypes.float8_e4m3fn).astype(np.float64) * np.repeat(np.exp2(scales.astype(np.float64) - 127.0), 8, axis=1)[..., None]
    return vals.transpose(0, 1, 3, 2).reshape(g * 512, n)


E2M1 = np.array([0.0, 0.5, 1.0, 1.5, 2.0, 3.0, 4.0, 6.0, -0.0, -0.5, -1.0, -1.5, -2.0, -3.0, -4.0, -6.0])


def pack_fp4(w):
    k, n = w.shape
    w = f64(np.asarray(w, np.float32).astype(ml_dtypes.bfloat16)).reshape(k // 32, 32, n)
    amax = np.abs(w).max(1)
    mant, ex = np.frexp(amax / 6.0)
    byte = np.clip(np.where(amax > 0, np.where(mant > 0.5, ex, ex - 1) + 127, 1), 1, 254)
    scaled = (w * np.exp2(127.0 - byte)[:, None, :]).reshape(k, n).astype(np.float32)
    c = np.ascontiguousarray(scaled.reshape(k // 512, 128, 4, n).transpose(0, 1, 3, 2)).astype(ml_dtypes.float4_e2m1fn).view(np.uint8) & 0xF
    words = (c[..., 0::2] | (c[..., 1::2] << 4)).reshape(k // 512, 128, 2 * n)
    return np.ascontiguousarray(words), np.ascontiguousarray(byte.astype(np.uint8).reshape(k // 512, 16, n))


def unpack_fp4(words, scales):
    g, _, n = scales.shape
    words = np.ascontiguousarray(words).reshape(g, 128, n, 2)
    nib = np.empty((g, 128, n, 4), np.uint8)
    nib[..., 0::2] = words & 0xF
    nib[..., 1::2] = words >> 4
    vals = E2M1[nib] * np.repeat(np.exp2(scales.astype(np.float64) - 127.0), 8, axis=1)[..., None]
    return vals.transpose(0, 1, 3, 2).reshape(g * 512, n)


def relu(v):
    return np.maximum(v, 0.0)

def planes(y):
    n, m = y.shape
    v = y.astype(np.float32).astype(ml_dtypes.bfloat16).astype(np.float64).reshape(n // 32, 32, m)
    top = np.abs(v).max(1)
    byte = np.clip(np.where(top > 0, np.frexp(top)[1] - 1 + 127 - 7, 1), 1, 254)
    codes = (v * np.exp2(127.0 - byte)[:, None, :]).reshape(n, m).astype(np.float32).astype(ml_dtypes.float8_e4m3fn).view(np.uint8)
    words = codes.reshape(n // 512, 128, 4, m).transpose(0, 1, 3, 2)
    return np.ascontiguousarray(words), np.ascontiguousarray(byte.astype(np.uint8).reshape(n // 512, 16, m))


K, T, S, V, H = 512, 2048, 512, 512, 512


def setup_inputs():
    n = np.random.standard_normal
    s = mx_kscale(K)[:, None]
    u = mx_kscale(S)
    packed_xT = pack_weight(n((K, T)) * s)
    packed_w1 = pack_fp4(n((K, H)) / np.sqrt(K) / s)
    packed_w2 = pack_fp4(n((K, H)) / np.sqrt(K) / s)
    return {
        "x_words": packed_xT[0],
        "x_scales": packed_xT[1],
        "w1_words": packed_w1[0],
        "w1_scales": packed_w1[1],
        "w2_words": packed_w2[0],
        "w2_scales": packed_w2[1],
        "ga": (np.random.uniform(0.5, 1.5, (H, 1)) * u[:, None]).astype(np.float32),
        "gb": (np.random.uniform(0.5, 1.5, (H, 1)) / u[:, None]).astype(np.float32),
        "offs": striped8(np.random.randint(0, T, (8, S))),
        "two": striped(np.random.permutation(T)[:V]),
        "n1": striped(np.random.permutation(S)),
        "n2": striped(np.random.permutation(S)),
        "n3": striped(np.random.permutation(V)),
        "n4": striped(np.random.permutation(V)),
        "n5": striped(np.random.permutation(V)),
        "n6": striped(np.random.permutation(V)),
    }


def reference(x_words, x_scales, w1_words, w1_scales, w2_words, w2_scales, ga, gb, offs, two, n1, n2, n3, n4, n5, n6):
    xq = unpack_weight(x_words, x_scales)[np.arange(K)[:, None], runs(offs, K)]
    a = unpack_fp4(w1_words, w1_scales).T @ xq
    z = f64(ga) * (a[:, unstriped(n1)] - a[:, unstriped(n2)])
    x_two = unpack_weight(x_words, x_scales)[:, unstriped(two)]
    b = unpack_fp4(w2_words, w2_scales).T @ x_two
    z2 = f64(gb) * (relu(b - b[:, unstriped(n3)]) + 0.5 * (relu(b[:, unstriped(n4)] - b)))
    s = 0.0625 * ((mxq(z, 0, "e4m3").T @ mxq(z2, 0, "e4m3")))
    ex = np.exp(s)
    out_0 = np.log(ex + ex[:, unstriped(n5)]) - s[:, unstriped(n6)]
    return (out_0,) + planes(out_0)

@@ -1,0 +1,253 @@
+from contextlib import ExitStack
+
+import concourse.mybir as mybir
+
+F32 = mybir.dt.float32
+BF16 = mybir.dt.bfloat16
+I32 = mybir.dt.int32
+U32 = mybir.dt.uint32
+U16 = mybir.dt.uint16
+U8 = mybir.dt.uint8
+FP8X4 = mybir.dt.float8_e4m3fn_x4
+FP4X4 = mybir.dt.float4_e2m1fn_x4
+ALU = mybir.AluOpType
+ACT = mybir.ActivationFunctionType
+
+P = 128
+PACK = 4
+TOKENS = 2048
+N = 512
+HALF = N // 2
+LIST_COLS = N // 16
+FUSED_B = 1
+FUSED_EX = 2
+
+FLOPS = 3 * 2 * N * N * N
+
+
+def tile_picked_hkqgaphingelse_none_po_kernel(
+    tc, x_words, x_scales, w1_words, w1_scales, w2_words, w2_scales, ga, gb,
+    offs, two, n1, n2, n3, n4, n5, n6, out_0, out_1, out_2,
+):
+    nc = tc.nc
+    with ExitStack() as ctx:
+        keep = ctx.enter_context(tc.tile_pool(name="keep", bufs=1))
+        psum = ctx.enter_context(tc.psum_pool(name="psum", bufs=1))
+
+        def sb(name, shape, dtype):
+            return keep.tile(shape, dtype, name=name, align_bytes=64)
+
+        def load_list(name, src):
+            tile = sb(name, [P, LIST_COLS], U16)
+            nc.sync.dma_start(tile[:], src)
+            return tile
+
+        def half_of(lst, h):
+            return lst[:, h * (LIST_COLS // 2):(h + 1) * (LIST_COLS // 2)]
+
+        def cols(h):
+            return slice(h * HALF, (h + 1) * HALF)
+
+        def load_scale_rows(tile, src):
+            rows = src[0].bitcast(I32)
+            for q in range(4):
+                quad = rows[4 * q:4 * q + 4, :].unsqueeze(0).to_broadcast([8, 4, rows.shape[1]])
+                nc.sync.dma_start(tile[32 * q:32 * q + 32, :].bitcast(I32), quad)
+
+        def load_gain(name, src):
+            tile = sb(name, [P, PACK], F32)
+            with nc.allow_non_contiguous_dma(reason="one value a partition and feature tile"):
+                for e in range(2):
+                    nc.sync.dma_start(tile[e:P:2, :], src.rearrange("(a r e) o -> e a (r o)", r=PACK, e=2)[e])
+            return tile
+
+        def load_words(tile, src):
+            nc.sync.dma_start(tile[:].bitcast(I32), src.bitcast(I32))
+
+        xs = sb("xs", [P, TOKENS], U8)
+        ws_raw = sb("ws_raw", [P, N], U8)
+        ww_raw = sb("ww_raw", [P, 2 * N], U8)
+        two_t = load_list("two_t", two)
+        load_scale_rows(xs, x_scales)
+        xw = sb("xw", [P, TOKENS], U32)
+        load_words(xw, x_words[0].rearrange("p n t -> p (n t)"))
+        offs_t = load_list("offs_t", offs)
+        load_words(ww_raw, w2_words[0])
+        load_scale_rows(ws_raw, w2_scales)
+        gb_t = load_gain("gb_t", gb)
+        n3_t = load_list("n3_t", n3)
+        n4_t = load_list("n4_t", n4)
+        ga_t = load_gain("ga_t", ga)
+        n2_t = load_list("n2_t", n2)
+        n1_t = load_list("n1_t", n1)
+        n5_t = load_list("n5_t", n5)
+        n6_t = load_list("n6_t", n6)
+
+        gb_neg = sb("gb_neg", [P, PACK], F32)
+        gb_half = sb("gb_half", [P, PACK], F32)
+        nc.scalar.activation(gb_neg[:], gb_t[:], ACT.Copy, scale=-1.0)
+        nc.scalar.activation(gb_half[:], gb_t[:], ACT.Copy, scale=0.5)
+
+        def deal(name, words_raw, scales_raw):
+            words = sb(name + "_w", [P, 2 * N], U8)
+            scales = sb(name + "_s", [P, N], U8)
+            for dealt, raw, pair in ((words, words_raw, U32), (scales, scales_raw, U16)):
+                nc.scalar.copy(
+                    dealt[:].bitcast(pair).rearrange("p (r m) -> p r m", r=PACK),
+                    raw[:].bitcast(pair).rearrange("p (m r) -> p r m", r=PACK),
+                )
+            return words, scales
+
+        two_s = sb("two_s", [P, N], U8)
+        nc.vector.tensor_copy(two_s[:], xs[:].indirect(two_t[:]))
+        offs_s_raw = sb("offs_s_raw", [P, N], U8)
+        nc.vector.tensor_copy(offs_s_raw[:], xs[:].indirect(offs_t[:]))
+        offs_s = sb("offs_s", [P, N], U8)
+        nc.vector.tensor_copy(offs_s[:].bitcast(I32), offs_s_raw[:].bitcast(I32))
+        for e in range(2):
+            nc.sync.dma_start(offs_s[2 + e:P:32, :].bitcast(I32), offs_s_raw[18 + e:P:32, :].bitcast(I32))
+        w2w, w2s = deal("w2", ww_raw, ws_raw)
+        load_words(ww_raw, w1_words[0])
+        load_scale_rows(ws_raw, w1_scales)
+        two_w = sb("two_w", [P, N], U32)
+        nc.vector.tensor_copy(two_w[:], xw[:].indirect(two_t[:]))
+
+        def product(tag, r, words, scales, mov_w, mov_s):
+            bank = psum.tile([P, N], F32, name=f"{tag}{r}", tag=f"{tag}{r}")
+            nc.tensor.matmul_mx(
+                out=bank[:],
+                lhsT=words[:, 2 * P * r:2 * P * (r + 1)].bitcast(FP4X4),
+                lhsT_scale=scales[:, P * r:P * (r + 1)],
+                rhs=mov_w[:].bitcast(FP8X4), rhs_scale=mov_s[:], start=True, stop=True,
+            )
+            return bank
+
+        b_ps = [product("low", r, w2w, w2s, two_w, two_s) for r in range(PACK)]
+        offs_w = sb("offs_w", [P, N], U32)
+        nc.vector.tensor_copy(offs_w[:], xw[:].indirect(offs_t[:]))
+        w1w, w1s = deal("w1", ww_raw, ws_raw)
+        a_ps = [product("high", r, w1w, w1s, offs_w, offs_s) for r in range(PACK)]
+
+        b_sb = [sb(f"b{r}", [P, N], F32) for r in range(PACK)]
+        b_again = [sb(f"b_again{r}", [P, N], F32) for r in range(FUSED_B)]
+        z2_bf = sb("z2_bf", [P, N, PACK], BF16)
+        z2_w = sb("z2_w", [P, N], U32)
+        z2_s = sb("z2_s", [P, N], U8)
+        for h in range(2):
+            down = sb(f"down{h}", [P, PACK, HALF], F32)
+            up = sb(f"up{h}", [P, PACK, HALF], F32)
+            for r in range(PACK):
+                diff = sb(f"diff{h}_{r}", [P, 2, HALF], F32)
+                if h == 0:
+                    nc.scalar.copy(b_sb[r][:], b_ps[r][:])
+                if r < FUSED_B:
+                    if h == 0:
+                        nc.scalar.copy(b_again[r][:], b_ps[r][:])
+                    for j, lst in enumerate((n3_t, n4_t)):
+                        nc.vector.tensor_tensor(
+                            diff[:, j, :], b_sb[r][:].indirect(half_of(lst, h)), b_again[r][:, cols(h)], ALU.subtract
+                        )
+                else:
+                    got = sb(f"got{h}_{r}", [P, 2, HALF], F32)
+                    for j, lst in enumerate((n3_t, n4_t)):
+                        nc.scalar.activation(got[:, j, :], b_sb[r][:].indirect(half_of(lst, h)), ACT.Copy)
+                    nc.vector.tensor_tensor(
+                        diff[:], got[:], b_sb[r][:, cols(h)].unsqueeze(1).to_broadcast([P, 2, HALF]), ALU.subtract
+                    )
+                nc.vector.tensor_scalar(down[:, r, :], diff[:, 0, :], 0.0, gb_neg[:, r:r + 1], ALU.min, ALU.mult)
+                nc.vector.tensor_scalar(up[:, r, :], diff[:, 1, :], 0.0, gb_half[:, r:r + 1], ALU.max, ALU.mult)
+            nc.vector.tensor_tensor(
+                z2_bf[:, cols(h), :].rearrange("p (c i) r -> p c r i", i=2),
+                down[:].rearrange("p r (c i) -> p c r i", i=2),
+                up[:].rearrange("p r (c i) -> p c r i", i=2),
+                ALU.add,
+            )
+            nc.vector.quantize_mx(
+                out=z2_w[:, cols(h)].bitcast(FP8X4), scales=z2_s[:, cols(h)],
+                in_=z2_bf[:, cols(h), :].rearrange("p c r -> p (c r)"),
+            )
+
+        a_sb = [sb(f"a{r}", [P, N], F32) for r in range(PACK)]
+        z_bf = sb("z_bf", [P, PACK, P, PACK], BF16)
+        for h in range(2):
+            z_f = sb(f"z_f{h}", [P, PACK, HALF], F32)
+            for r in range(PACK):
+                if h == 0:
+                    nc.scalar.activation(a_sb[r][:], a_ps[r][:], ACT.Copy, scale=ga_t[:, r:r + 1])
+                a_n2 = sb(f"a_n2_{h}_{r}", [P, HALF], F32)
+                nc.scalar.activation(a_n2[:], a_sb[r][:].indirect(half_of(n2_t, h)), ACT.Copy)
+                nc.vector.tensor_tensor(z_f[:, r, :], a_sb[r][:].indirect(half_of(n1_t, h)), a_n2[:], ALU.subtract)
+            nc.vector.tensor_copy(
+                z_bf[:, :, h * (P // 2):(h + 1) * (P // 2), :].rearrange("p t m r -> p m t r"),
+                z_f[:].rearrange("p r (m t) -> p m t r", t=PACK),
+            )
+
+        ex, s_neg = [], []
+        for t in range(PACK):
+            z_w = sb(f"z_w{t}", [P, P], U32)
+            z_s = sb(f"z_s{t}", [P, P], U8)
+            nc.vector.quantize_mx(out=z_w[:].bitcast(FP8X4), scales=z_s[:], in_=z_bf[:, t].rearrange("p m r -> p (m r)"))
+            bank = psum.tile([P, N], F32, name=f"s{t}", tag=f"low{t}")
+            nc.tensor.matmul_mx(
+                out=bank[:], lhsT=z_w[:].bitcast(FP8X4), lhsT_scale=z_s[:],
+                rhs=z2_w[:].bitcast(FP8X4), rhs_scale=z2_s[:], start=True, stop=True,
+            )
+            ex.append(sb(f"ex{t}", [P, N], F32))
+            nc.scalar.activation(ex[t][:], bank[:], ACT.Exp, scale=0.0625)
+            s_neg.append((sb(f"s_neg{t}", [P, N], F32), bank))
+
+        def negate(t):
+            tile, bank = s_neg[t]
+            if t < PACK - 1:
+                nc.vector.tensor_scalar(tile[:], bank[:], -0.0625, None, ALU.mult)
+            else:
+                nc.scalar.activation(tile[:], bank[:], ACT.Copy, scale=-0.0625)
+
+        logs = []
+        for t in range(PACK):
+            total = sb(f"total{t}", [P, N], F32)
+            negate(t)
+            if t < FUSED_EX:
+                ex_again = sb(f"ex_again{t}", [P, N], F32)
+                nc.vector.tensor_copy(ex_again[:], ex[t][:])
+                for h in range(2):
+                    nc.vector.tensor_tensor(total[:, cols(h)], ex[t][:].indirect(half_of(n5_t, h)), ex_again[:, cols(h)], ALU.add)
+            else:
+                ex_n5 = sb(f"ex_n5_{t}", [P, N], F32)
+                for h in range(2):
+                    nc.scalar.activation(ex_n5[:, cols(h)], ex[t][:].indirect(half_of(n5_t, h)), ACT.Copy)
+                nc.vector.tensor_tensor(total[:], ex_n5[:], ex[t][:], ALU.add)
+            logs.append(sb(f"log{t}", [P, N], F32))
+            nc.scalar.activation(logs[t][:], total[:], ACT.Ln)
+
+        out_rows = out_0.rearrange("(p t) v -> p t v", t=PACK)
+        out_words = out_1[0].rearrange("p n t -> p (n t)").bitcast(I32)
+        y_s = sb("y_s", [P, N], U8)
+        y_half = [sb(f"y{h}", [P, PACK, HALF], F32) for h in range(2)]
+
+        def finish(t, h):
+            nc.vector.tensor_tensor(y_half[h][:, t, :], s_neg[t][0][:].indirect(half_of(n6_t, h)), logs[t][:, cols(h)], ALU.add)
+            nc.sync.dma_start(out_rows[:, t, cols(h)], y_half[h][:, t, :])
+
+        def planes(h):
+            y_bf = sb(f"y_bf{h}", [P, HALF, PACK], BF16)
+            if h == 0:
+                nc.scalar.copy(y_bf[:], y_half[h][:].rearrange("p t c -> p c t"))
+            else:
+                nc.vector.tensor_copy(y_bf[:], y_half[h][:].rearrange("p t c -> p c t"))
+            y_w = sb(f"y_w{h}", [P, HALF], U32)
+            nc.vector.quantize_mx(out=y_w[:].bitcast(FP8X4), scales=y_s[:, cols(h)], in_=y_bf[:].rearrange("p c t -> p (c t)"))
+            nc.sync.dma_start(out_words[:, cols(h)], y_w[:].bitcast(I32))
+
+        for t in range(PACK - 2):
+            finish(t, 0)
+            finish(t, 1)
+        finish(2, 0)
+        finish(3, 0)
+        finish(2, 1)
+        finish(3, 1)
+        planes(0)
+        planes(1)
+        scale_rows = out_2[0].bitcast(I32).rearrange("(q i) n -> i q n", i=4)
+        for i in range(4):
+            nc.scalar.dma_start(scale_rows[i], y_s[i:P:32, :].bitcast(I32))

@@ -19,8 +19,9 @@ TOKENS = 2048
 N = 512
 HALF = N // 2
 LIST_COLS = N // 16
-FUSED_B = 1
+WINDOW = N + 8
 FUSED_EX = 2
+NEG_ON_VECTOR = 1
 
 FLOPS = 3 * 2 * N * N * N
 
@@ -34,8 +35,13 @@ def tile_picked_hkqgaphingelse_none_po_kernel(
         keep = ctx.enter_context(tc.tile_pool(name="keep", bufs=1))
         psum = ctx.enter_context(tc.psum_pool(name="psum", bufs=1))
 
-        def sb(name, shape, dtype):
-            return keep.tile(shape, dtype, name=name, align_bytes=64)
+        def sb(name, shape, dtype, tag=None):
+            return keep.tile(shape, dtype, name=name, tag=tag or name, align_bytes=64)
+
+        def window(name):
+            tile = sb(name, [P, WINDOW], F32)
+            nc.gpsimd.memset(tile[:, N:], 0.0)
+            return tile
 
         def load_list(name, src):
             tile = sb(name, [P, LIST_COLS], U16)
@@ -65,21 +71,26 @@ def tile_picked_hkqgaphingelse_none_po_kernel(
             nc.sync.dma_start(tile[:].bitcast(I32), src.bitcast(I32))
 
         xs = sb("xs", [P, TOKENS], U8)
-        ws_raw = sb("ws_raw", [P, N], U8)
-        ww_raw = sb("ww_raw", [P, 2 * N], U8)
-        two_t = load_list("two_t", two)
-        load_scale_rows(xs, x_scales)
         xw = sb("xw", [P, TOKENS], U32)
-        load_words(xw, x_words[0].rearrange("p n t -> p (n t)"))
+        w2s_raw = sb("w2s_raw", [P, N], U8)
+        w2w_raw = sb("w2w_raw", [P, 2 * N], U8)
+        w1_raw = sb("w1_raw", [P, 3 * N], U8)
+        w1w_raw = w1_raw[:, :2 * N]
+        w1s_raw = w1_raw[:, 2 * N:]
         offs_t = load_list("offs_t", offs)
-        load_words(ww_raw, w2_words[0])
-        load_scale_rows(ws_raw, w2_scales)
+        load_scale_rows(xs, x_scales)
+        two_t = load_list("two_t", two)
+        load_words(xw, x_words[0].rearrange("p n t -> p (n t)"))
+        load_words(w2w_raw, w2_words[0])
+        load_scale_rows(w2s_raw, w2_scales)
         gb_t = load_gain("gb_t", gb)
         n3_t = load_list("n3_t", n3)
         n4_t = load_list("n4_t", n4)
+        load_words(w1w_raw, w1_words[0])
+        load_scale_rows(w1s_raw, w1_scales)
         ga_t = load_gain("ga_t", ga)
-        n2_t = load_list("n2_t", n2)
         n1_t = load_list("n1_t", n1)
+        n2_t = load_list("n2_t", n2)
         n5_t = load_list("n5_t", n5)
         n6_t = load_list("n6_t", n6)
 
@@ -98,156 +109,137 @@ def tile_picked_hkqgaphingelse_none_po_kernel(
                 )
             return words, scales
 
-        two_s = sb("two_s", [P, N], U8)
-        nc.vector.tensor_copy(two_s[:], xs[:].indirect(two_t[:]))
         offs_s_raw = sb("offs_s_raw", [P, N], U8)
         nc.vector.tensor_copy(offs_s_raw[:], xs[:].indirect(offs_t[:]))
+        two_s = sb("two_s", [P, N], U8)
+        nc.vector.tensor_copy(two_s[:], xs[:].indirect(two_t[:]))
         offs_s = sb("offs_s", [P, N], U8)
         nc.vector.tensor_copy(offs_s[:].bitcast(I32), offs_s_raw[:].bitcast(I32))
         for e in range(2):
-            nc.sync.dma_start(offs_s[2 + e:P:32, :].bitcast(I32), offs_s_raw[18 + e:P:32, :].bitcast(I32))
-        w2w, w2s = deal("w2", ww_raw, ws_raw)
-        load_words(ww_raw, w1_words[0])
-        load_scale_rows(ws_raw, w1_scales)
+            nc.gpsimd.dma_start(offs_s[2 + e:P:32, :].bitcast(I32), offs_s_raw[18 + e:P:32, :].bitcast(I32))
+        w2w, w2s = deal("w2", w2w_raw, w2s_raw)
         two_w = sb("two_w", [P, N], U32)
-        nc.vector.tensor_copy(two_w[:], xw[:].indirect(two_t[:]))
 
         def product(tag, r, words, scales, mov_w, mov_s):
-            bank = psum.tile([P, N], F32, name=f"{tag}{r}", tag=f"{tag}{r}")
+            bank = psum.tile([P, mov_s.shape[1]], F32, name=tag, tag=tag)
             nc.tensor.matmul_mx(
                 out=bank[:],
                 lhsT=words[:, 2 * P * r:2 * P * (r + 1)].bitcast(FP4X4),
                 lhsT_scale=scales[:, P * r:P * (r + 1)],
-                rhs=mov_w[:].bitcast(FP8X4), rhs_scale=mov_s[:], start=True, stop=True,
+                rhs=mov_w.bitcast(FP8X4), rhs_scale=mov_s, start=True, stop=True,
             )
             return bank
 
-        b_ps = [product("low", r, w2w, w2s, two_w, two_s) for r in range(PACK)]
+        b_first = []
+        for h, tag in enumerate(("low0", "high0")):
+            nc.vector.tensor_copy(two_w[:, cols(h)], xw[:].indirect(half_of(two_t, h)))
+            b_first.append((cols(h), product(tag, 0, w2w, w2s, two_w[:, cols(h)], two_s[:, cols(h)])))
+        b_ps = [b_first] + [[(slice(0, N), product(f"low{r}", r, w2w, w2s, two_w[:], two_s[:]))] for r in range(1, PACK)]
         offs_w = sb("offs_w", [P, N], U32)
         nc.vector.tensor_copy(offs_w[:], xw[:].indirect(offs_t[:]))
-        w1w, w1s = deal("w1", ww_raw, ws_raw)
-        a_ps = [product("high", r, w1w, w1s, offs_w, offs_s) for r in range(PACK)]
 
-        b_sb = [sb(f"b{r}", [P, N], F32) for r in range(PACK)]
-        b_again = [sb(f"b_again{r}", [P, N], F32) for r in range(FUSED_B)]
+        w1w, w1s = deal("w1", w1w_raw, w1s_raw)
+
+        down = sb("down", [P, PACK, N], F32)
+        up = sb("up", [P, PACK, N], F32)
+        for r in range(PACK):
+            b_sb = window(f"b{r}")
+            b_neg = sb(f"b_neg{r}", [P, N], F32, tag="w1_raw" if r == 2 else None)
+            diff = sb(f"diff{r}", [P, 2, N], F32)
+            for where, bank in b_ps[r]:
+                nc.scalar.copy(b_sb[:, where], bank[:])
+                nc.scalar.activation(b_neg[:, where], bank[:], ACT.Copy, scale=-1.0)
+            for j, lst in enumerate((n3_t, n4_t)):
+                nc.vector.tensor_tensor(diff[:, j, :], b_sb[:].indirect(lst[:]), b_neg[:], ALU.add)
+            nc.vector.tensor_scalar(down[:, r, :], diff[:, 0, :], 0.0, gb_neg[:, r:r + 1], ALU.min, ALU.mult)
+            nc.vector.tensor_scalar(up[:, r, :], diff[:, 1, :], 0.0, gb_half[:, r:r + 1], ALU.max, ALU.mult)
         z2_bf = sb("z2_bf", [P, N, PACK], BF16)
         z2_w = sb("z2_w", [P, N], U32)
         z2_s = sb("z2_s", [P, N], U8)
-        for h in range(2):
-            down = sb(f"down{h}", [P, PACK, HALF], F32)
-            up = sb(f"up{h}", [P, PACK, HALF], F32)
-            for r in range(PACK):
-                diff = sb(f"diff{h}_{r}", [P, 2, HALF], F32)
-                if h == 0:
-                    nc.scalar.copy(b_sb[r][:], b_ps[r][:])
-                if r < FUSED_B:
-                    if h == 0:
-                        nc.scalar.copy(b_again[r][:], b_ps[r][:])
-                    for j, lst in enumerate((n3_t, n4_t)):
-                        nc.vector.tensor_tensor(
-                            diff[:, j, :], b_sb[r][:].indirect(half_of(lst, h)), b_again[r][:, cols(h)], ALU.subtract
-                        )
-                else:
-                    got = sb(f"got{h}_{r}", [P, 2, HALF], F32)
-                    for j, lst in enumerate((n3_t, n4_t)):
-                        nc.scalar.activation(got[:, j, :], b_sb[r][:].indirect(half_of(lst, h)), ACT.Copy)
-                    nc.vector.tensor_tensor(
-                        diff[:], got[:], b_sb[r][:, cols(h)].unsqueeze(1).to_broadcast([P, 2, HALF]), ALU.subtract
-                    )
-                nc.vector.tensor_scalar(down[:, r, :], diff[:, 0, :], 0.0, gb_neg[:, r:r + 1], ALU.min, ALU.mult)
-                nc.vector.tensor_scalar(up[:, r, :], diff[:, 1, :], 0.0, gb_half[:, r:r + 1], ALU.max, ALU.mult)
-            nc.vector.tensor_tensor(
-                z2_bf[:, cols(h), :].rearrange("p (c i) r -> p c r i", i=2),
-                down[:].rearrange("p r (c i) -> p c r i", i=2),
-                up[:].rearrange("p r (c i) -> p c r i", i=2),
-                ALU.add,
-            )
-            nc.vector.quantize_mx(
-                out=z2_w[:, cols(h)].bitcast(FP8X4), scales=z2_s[:, cols(h)],
-                in_=z2_bf[:, cols(h), :].rearrange("p c r -> p (c r)"),
-            )
+        nc.vector.tensor_tensor(
+            z2_bf[:].rearrange("p (c i) r -> p c r i", i=2),
+            down[:].rearrange("p r (c i) -> p c r i", i=2),
+            up[:].rearrange("p r (c i) -> p c r i", i=2),
+            ALU.add,
+        )
 
-        a_sb = [sb(f"a{r}", [P, N], F32) for r in range(PACK)]
+        nc.vector.quantize_mx(out=z2_w[:].bitcast(FP8X4), scales=z2_s[:], in_=z2_bf[:].rearrange("p c r -> p (c r)"))
+
+        a_ps = [product(f"high{r}", r, w1w, w1s, offs_w[:], offs_s[:]) for r in range(PACK)]
+        a_n1 = sb("a_n1", [P, PACK, N], F32)
+        a_n2 = sb("a_n2", [P, PACK, N], F32)
         z_bf = sb("z_bf", [P, PACK, P, PACK], BF16)
+        for r in range(PACK):
+            a_sb = window(f"a{r}")
+            nc.scalar.activation(a_sb[:, :N], a_ps[r][:], ACT.Copy, scale=ga_t[:, r:r + 1])
+            if r < PACK - 1:
+                for got, lst in ((a_n1, n1_t), (a_n2, n2_t)):
+                    nc.scalar.activation(got[:, r, :], a_sb[:].indirect(lst[:]), ACT.Copy)
+            else:
+                for h in range(2):
+                    for got, lst in ((a_n1, n1_t), (a_n2, n2_t)):
+                        nc.scalar.activation(got[:, r, cols(h)], a_sb[:].indirect(half_of(lst, h)), ACT.Copy)
         for h in range(2):
-            z_f = sb(f"z_f{h}", [P, PACK, HALF], F32)
-            for r in range(PACK):
-                if h == 0:
-                    nc.scalar.activation(a_sb[r][:], a_ps[r][:], ACT.Copy, scale=ga_t[:, r:r + 1])
-                a_n2 = sb(f"a_n2_{h}_{r}", [P, HALF], F32)
-                nc.scalar.activation(a_n2[:], a_sb[r][:].indirect(half_of(n2_t, h)), ACT.Copy)
-                nc.vector.tensor_tensor(z_f[:, r, :], a_sb[r][:].indirect(half_of(n1_t, h)), a_n2[:], ALU.subtract)
-            nc.vector.tensor_copy(
-                z_bf[:, :, h * (P // 2):(h + 1) * (P // 2), :].rearrange("p t m r -> p m t r"),
-                z_f[:].rearrange("p r (m t) -> p m t r", t=PACK),
+            nc.vector.tensor_tensor(
+                z_bf[:, :, h * (P // 2):(h + 1) * (P // 2), :].rearrange("p t m r -> p m r t"),
+                a_n1[:, :, cols(h)].rearrange("p r (m t) -> p m r t", t=PACK),
+                a_n2[:, :, cols(h)].rearrange("p r (m t) -> p m r t", t=PACK),
+                ALU.subtract,
             )
 
-        ex, s_neg = [], []
+        ex, s_ps = [], []
         for t in range(PACK):
             z_w = sb(f"z_w{t}", [P, P], U32)
             z_s = sb(f"z_s{t}", [P, P], U8)
             nc.vector.quantize_mx(out=z_w[:].bitcast(FP8X4), scales=z_s[:], in_=z_bf[:, t].rearrange("p m r -> p (m r)"))
-            bank = psum.tile([P, N], F32, name=f"s{t}", tag=f"low{t}")
+            s_ps.append(psum.tile([P, N], F32, name=f"s{t}", tag=f"low{t}"))
             nc.tensor.matmul_mx(
-                out=bank[:], lhsT=z_w[:].bitcast(FP8X4), lhsT_scale=z_s[:],
+                out=s_ps[t][:], lhsT=z_w[:].bitcast(FP8X4), lhsT_scale=z_s[:],
                 rhs=z2_w[:].bitcast(FP8X4), rhs_scale=z2_s[:], start=True, stop=True,
             )
-            ex.append(sb(f"ex{t}", [P, N], F32))
-            nc.scalar.activation(ex[t][:], bank[:], ACT.Exp, scale=0.0625)
-            s_neg.append((sb(f"s_neg{t}", [P, N], F32), bank))
+            ex.append(window(f"ex{t}"))
+            nc.scalar.activation(ex[t][:, :N], s_ps[t][:], ACT.Exp, scale=0.0625)
 
-        def negate(t):
-            tile, bank = s_neg[t]
-            if t < PACK - 1:
-                nc.vector.tensor_scalar(tile[:], bank[:], -0.0625, None, ALU.mult)
-            else:
-                nc.scalar.activation(tile[:], bank[:], ACT.Copy, scale=-0.0625)
-
-        logs = []
+        logs, s_neg = [], []
         for t in range(PACK):
             total = sb(f"total{t}", [P, N], F32)
-            negate(t)
+            s_neg.append(window(f"s_neg{t}"))
+            if t == 0:
+                nc.vector.tensor_scalar(s_neg[t][:, :N], s_ps[t][:], -0.0625, None, ALU.mult)
             if t < FUSED_EX:
                 ex_again = sb(f"ex_again{t}", [P, N], F32)
-                nc.vector.tensor_copy(ex_again[:], ex[t][:])
-                for h in range(2):
-                    nc.vector.tensor_tensor(total[:, cols(h)], ex[t][:].indirect(half_of(n5_t, h)), ex_again[:, cols(h)], ALU.add)
+                nc.vector.tensor_copy(ex_again[:], ex[t][:, :N])
+                nc.vector.tensor_tensor(total[:], ex[t][:].indirect(n5_t[:]), ex_again[:], ALU.add)
             else:
                 ex_n5 = sb(f"ex_n5_{t}", [P, N], F32)
-                for h in range(2):
-                    nc.scalar.activation(ex_n5[:, cols(h)], ex[t][:].indirect(half_of(n5_t, h)), ACT.Copy)
-                nc.vector.tensor_tensor(total[:], ex_n5[:], ex[t][:], ALU.add)
+                nc.scalar.activation(ex_n5[:], ex[t][:].indirect(n5_t[:]), ACT.Copy)
+                nc.vector.tensor_tensor(total[:], ex_n5[:], ex[t][:, :N], ALU.add)
+            if 0 < t < NEG_ON_VECTOR:
+                nc.vector.tensor_scalar(s_neg[t][:, :N], s_ps[t][:], -0.0625, None, ALU.mult)
+            if t >= NEG_ON_VECTOR:
+                nc.scalar.activation(s_neg[t][:, :N], s_ps[t][:], ACT.Copy, scale=-0.0625)
             logs.append(sb(f"log{t}", [P, N], F32))
-            nc.scalar.activation(logs[t][:], total[:], ACT.Ln)
+            for where in ([slice(0, N)] if t < PACK - 1 else [cols(0), cols(1)]):
+                nc.scalar.activation(logs[t][:, where], total[:, where], ACT.Ln)
 
         out_rows = out_0.rearrange("(p t) v -> p t v", t=PACK)
         out_words = out_1[0].rearrange("p n t -> p (n t)").bitcast(I32)
-        y_s = sb("y_s", [P, N], U8)
-        y_half = [sb(f"y{h}", [P, PACK, HALF], F32) for h in range(2)]
-
-        def finish(t, h):
-            nc.vector.tensor_tensor(y_half[h][:, t, :], s_neg[t][0][:].indirect(half_of(n6_t, h)), logs[t][:, cols(h)], ALU.add)
-            nc.sync.dma_start(out_rows[:, t, cols(h)], y_half[h][:, t, :])
-
-        def planes(h):
-            y_bf = sb(f"y_bf{h}", [P, HALF, PACK], BF16)
-            if h == 0:
-                nc.scalar.copy(y_bf[:], y_half[h][:].rearrange("p t c -> p c t"))
+        y = sb("y", [P, PACK, N], F32)
+        for t in range(PACK):
+            if t < PACK - 1:
+                nc.vector.tensor_tensor(y[:, t, :], s_neg[t][:].indirect(n6_t[:]), logs[t][:], ALU.add)
             else:
-                nc.vector.tensor_copy(y_bf[:], y_half[h][:].rearrange("p t c -> p c t"))
+                for h in range(2):
+                    nc.vector.tensor_tensor(y[:, t, cols(h)], s_neg[t][:].indirect(half_of(n6_t, h)), logs[t][:, cols(h)], ALU.add)
+            nc.sync.dma_start(out_rows[:, t, :], y[:, t, :])
+        y_bf = [sb(f"y_bf{h}", [P, HALF, PACK], BF16) for h in range(2)]
+        for h, copy in enumerate((nc.scalar.copy, nc.vector.tensor_copy)):
+            copy(y_bf[h][:].rearrange("p (c i) t -> p c t i", i=4), y[:, :, cols(h)].rearrange("p t (c i) -> p c t i", i=4))
+        y_s = sb("y_s", [P, N], U8)
+        for h in range(2):
             y_w = sb(f"y_w{h}", [P, HALF], U32)
-            nc.vector.quantize_mx(out=y_w[:].bitcast(FP8X4), scales=y_s[:, cols(h)], in_=y_bf[:].rearrange("p c t -> p (c t)"))
+            nc.vector.quantize_mx(out=y_w[:].bitcast(FP8X4), scales=y_s[:, cols(h)], in_=y_bf[h][:].rearrange("p c t -> p (c t)"))
             nc.sync.dma_start(out_words[:, cols(h)], y_w[:].bitcast(I32))
-
-        for t in range(PACK - 2):
-            finish(t, 0)
-            finish(t, 1)
-        finish(2, 0)
-        finish(3, 0)
-        finish(2, 1)
-        finish(3, 1)
-        planes(0)
-        planes(1)
         scale_rows = out_2[0].bitcast(I32).rearrange("(q i) n -> i q n", i=4)
         for i in range(4):
             nc.scalar.dma_start(scale_rows[i], y_s[i:P:32, :].bitcast(I32))

@@ -228,13 +228,14 @@ def tile_picked_hkqgaphingelse_none_po_kernel(
         for t in range(PACK):
             if t < PACK - 1:
                 nc.vector.tensor_tensor(y[:, t, :], s_neg[t][:].indirect(n6_t[:]), logs[t][:], ALU.add)
+                nc.sync.dma_start(out_rows[:, t, :], y[:, t, :])
             else:
                 for h in range(2):
                     nc.vector.tensor_tensor(y[:, t, cols(h)], s_neg[t][:].indirect(half_of(n6_t, h)), logs[t][:, cols(h)], ALU.add)
-            nc.sync.dma_start(out_rows[:, t, :], y[:, t, :])
+                    nc.sync.dma_start(out_rows[:, t, cols(h)], y[:, t, cols(h)])
         y_bf = [sb(f"y_bf{h}", [P, HALF, PACK], BF16) for h in range(2)]
         for h, copy in enumerate((nc.scalar.copy, nc.vector.tensor_copy)):
-            copy(y_bf[h][:].rearrange("p (c i) t -> p c t i", i=4), y[:, :, cols(h)].rearrange("p t (c i) -> p c t i", i=4))
+            copy(y_bf[h][:], y[:, :, cols(h)].rearrange("p t c -> p c t"))
         y_s = sb("y_s", [P, N], U8)
         for h in range(2):
             y_w = sb(f"y_w{h}", [P, HALF], U32)

from contextlib import ExitStack

import concourse.mybir as mybir

F32 = mybir.dt.float32
BF16 = mybir.dt.bfloat16
I32 = mybir.dt.int32
U32 = mybir.dt.uint32
U16 = mybir.dt.uint16
U8 = mybir.dt.uint8
FP8X4 = mybir.dt.float8_e4m3fn_x4
FP4X4 = mybir.dt.float4_e2m1fn_x4
ALU = mybir.AluOpType
ACT = mybir.ActivationFunctionType

P = 128
PACK = 4
TOKENS = 2048
N = 512
HALF = N // 2
LIST_COLS = N // 16
WINDOW = N + 8
FUSED_EX = 2
NEG_ON_VECTOR = 1

FLOPS = 3 * 2 * N * N * N


def tile_picked_hkqgaphingelse_none_po_kernel(
    tc, x_words, x_scales, w1_words, w1_scales, w2_words, w2_scales, ga, gb,
    offs, two, n1, n2, n3, n4, n5, n6, out_0, out_1, out_2,
):
    nc = tc.nc
    with ExitStack() as ctx:
        keep = ctx.enter_context(tc.tile_pool(name="keep", bufs=1))
        psum = ctx.enter_context(tc.psum_pool(name="psum", bufs=1))

        def sb(name, shape, dtype, tag=None):
            return keep.tile(shape, dtype, name=name, tag=tag or name, align_bytes=64)

        def window(name):
            tile = sb(name, [P, WINDOW], F32)
            nc.gpsimd.memset(tile[:, N:], 0.0)
            return tile

        def load_list(name, src):
            tile = sb(name, [P, LIST_COLS], U16)
            nc.sync.dma_start(tile[:], src)
            return tile

        def half_of(lst, h):
            return lst[:, h * (LIST_COLS // 2):(h + 1) * (LIST_COLS // 2)]

        def cols(h):
            return slice(h * HALF, (h + 1) * HALF)

        def load_scale_rows(tile, src):
            rows = src[0].bitcast(I32)
            for q in range(4):
                quad = rows[4 * q:4 * q + 4, :].unsqueeze(0).to_broadcast([8, 4, rows.shape[1]])
                nc.sync.dma_start(tile[32 * q:32 * q + 32, :].bitcast(I32), quad)

        def load_gain(name, src):
            tile = sb(name, [P, PACK], F32)
            with nc.allow_non_contiguous_dma(reason="one value a partition and feature tile"):
                for e in range(2):
                    nc.sync.dma_start(tile[e:P:2, :], src.rearrange("(a r e) o -> e a (r o)", r=PACK, e=2)[e])
            return tile

        def load_words(tile, src):
            nc.sync.dma_start(tile[:].bitcast(I32), src.bitcast(I32))

        xs = sb("xs", [P, TOKENS], U8)
        xw = sb("xw", [P, TOKENS], U32)
        w2s_raw = sb("w2s_raw", [P, N], U8)
        w2w_raw = sb("w2w_raw", [P, 2 * N], U8)
        w1_raw = sb("w1_raw", [P, 3 * N], U8)
        w1w_raw = w1_raw[:, :2 * N]
        w1s_raw = w1_raw[:, 2 * N:]
        offs_t = load_list("offs_t", offs)
        load_scale_rows(xs, x_scales)
        two_t = load_list("two_t", two)
        load_words(xw, x_words[0].rearrange("p n t -> p (n t)"))
        load_words(w2w_raw, w2_words[0])
        load_scale_rows(w2s_raw, w2_scales)
        gb_t = load_gain("gb_t", gb)
        n3_t = load_list("n3_t", n3)
        n4_t = load_list("n4_t", n4)
        load_words(w1w_raw, w1_words[0])
        load_scale_rows(w1s_raw, w1_scales)
        ga_t = load_gain("ga_t", ga)
        n1_t = load_list("n1_t", n1)
        n2_t = load_list("n2_t", n2)
        n5_t = load_list("n5_t", n5)
        n6_t = load_list("n6_t", n6)

        gb_neg = sb("gb_neg", [P, PACK], F32)
        gb_half = sb("gb_half", [P, PACK], F32)
        nc.scalar.activation(gb_neg[:], gb_t[:], ACT.Copy, scale=-1.0)
        nc.scalar.activation(gb_half[:], gb_t[:], ACT.Copy, scale=0.5)

        def deal(name, words_raw, scales_raw):
            words = sb(name + "_w", [P, 2 * N], U8)
            scales = sb(name + "_s", [P, N], U8)
            for dealt, raw, pair in ((words, words_raw, U32), (scales, scales_raw, U16)):
                nc.scalar.copy(
                    dealt[:].bitcast(pair).rearrange("p (r m) -> p r m", r=PACK),
                    raw[:].bitcast(pair).rearrange("p (m r) -> p r m", r=PACK),
                )
            return words, scales

        offs_s_raw = sb("offs_s_raw", [P, N], U8)
        nc.vector.tensor_copy(offs_s_raw[:], xs[:].indirect(offs_t[:]))
        two_s = sb("two_s", [P, N], U8)
        nc.vector.tensor_copy(two_s[:], xs[:].indirect(two_t[:]))
        offs_s = sb("offs_s", [P, N], U8)
        nc.vector.tensor_copy(offs_s[:].bitcast(I32), offs_s_raw[:].bitcast(I32))
        for e in range(2):
            nc.gpsimd.dma_start(offs_s[2 + e:P:32, :].bitcast(I32), offs_s_raw[18 + e:P:32, :].bitcast(I32))
        w2w, w2s = deal("w2", w2w_raw, w2s_raw)
        two_w = sb("two_w", [P, N], U32)

        def product(tag, r, words, scales, mov_w, mov_s):
            bank = psum.tile([P, mov_s.shape[1]], F32, name=tag, tag=tag)
            nc.tensor.matmul_mx(
                out=bank[:],
                lhsT=words[:, 2 * P * r:2 * P * (r + 1)].bitcast(FP4X4),
                lhsT_scale=scales[:, P * r:P * (r + 1)],
                rhs=mov_w.bitcast(FP8X4), rhs_scale=mov_s, start=True, stop=True,
            )
            return bank

        b_first = []
        for h, tag in enumerate(("low0", "high0")):
            nc.vector.tensor_copy(two_w[:, cols(h)], xw[:].indirect(half_of(two_t, h)))
            b_first.append((cols(h), product(tag, 0, w2w, w2s, two_w[:, cols(h)], two_s[:, cols(h)])))
        b_ps = [b_first] + [[(slice(0, N), product(f"low{r}", r, w2w, w2s, two_w[:], two_s[:]))] for r in range(1, PACK)]
        offs_w = sb("offs_w", [P, N], U32)
        nc.vector.tensor_copy(offs_w[:], xw[:].indirect(offs_t[:]))

        w1w, w1s = deal("w1", w1w_raw, w1s_raw)

        down = sb("down", [P, PACK, N], F32)
        up = sb("up", [P, PACK, N], F32)
        for r in range(PACK):
            b_sb = window(f"b{r}")
            b_neg = sb(f"b_neg{r}", [P, N], F32, tag="w1_raw" if r == 2 else None)
            diff = sb(f"diff{r}", [P, 2, N], F32)
            for where, bank in b_ps[r]:
                nc.scalar.copy(b_sb[:, where], bank[:])
                nc.scalar.activation(b_neg[:, where], bank[:], ACT.Copy, scale=-1.0)
            for j, lst in enumerate((n3_t, n4_t)):
                nc.vector.tensor_tensor(diff[:, j, :], b_sb[:].indirect(lst[:]), b_neg[:], ALU.add)
            nc.vector.tensor_scalar(down[:, r, :], diff[:, 0, :], 0.0, gb_neg[:, r:r + 1], ALU.min, ALU.mult)
            nc.vector.tensor_scalar(up[:, r, :], diff[:, 1, :], 0.0, gb_half[:, r:r + 1], ALU.max, ALU.mult)
        z2_bf = sb("z2_bf", [P, N, PACK], BF16)
        z2_w = sb("z2_w", [P, N], U32)
        z2_s = sb("z2_s", [P, N], U8)
        nc.vector.tensor_tensor(
            z2_bf[:].rearrange("p (c i) r -> p c r i", i=2),
            down[:].rearrange("p r (c i) -> p c r i", i=2),
            up[:].rearrange("p r (c i) -> p c r i", i=2),
            ALU.add,
        )

        nc.vector.quantize_mx(out=z2_w[:].bitcast(FP8X4), scales=z2_s[:], in_=z2_bf[:].rearrange("p c r -> p (c r)"))

        a_ps = [product(f"high{r}", r, w1w, w1s, offs_w[:], offs_s[:]) for r in range(PACK)]
        a_n1 = sb("a_n1", [P, PACK, N], F32)
        a_n2 = sb("a_n2", [P, PACK, N], F32)
        z_bf = sb("z_bf", [P, PACK, P, PACK], BF16)
        for r in range(PACK):
            a_sb = window(f"a{r}")
            nc.scalar.activation(a_sb[:, :N], a_ps[r][:], ACT.Copy, scale=ga_t[:, r:r + 1])
            if r < PACK - 1:
                for got, lst in ((a_n1, n1_t), (a_n2, n2_t)):
                    nc.scalar.activation(got[:, r, :], a_sb[:].indirect(lst[:]), ACT.Copy)
            else:
                for h in range(2):
                    for got, lst in ((a_n1, n1_t), (a_n2, n2_t)):
                        nc.scalar.activation(got[:, r, cols(h)], a_sb[:].indirect(half_of(lst, h)), ACT.Copy)
        for h in range(2):
            nc.vector.tensor_tensor(
                z_bf[:, :, h * (P // 2):(h + 1) * (P // 2), :].rearrange("p t m r -> p m r t"),
                a_n1[:, :, cols(h)].rearrange("p r (m t) -> p m r t", t=PACK),
                a_n2[:, :, cols(h)].rearrange("p r (m t) -> p m r t", t=PACK),
                ALU.subtract,
            )

        ex, s_ps = [], []
        for t in range(PACK):
            z_w = sb(f"z_w{t}", [P, P], U32)
            z_s = sb(f"z_s{t}", [P, P], U8)
            nc.vector.quantize_mx(out=z_w[:].bitcast(FP8X4), scales=z_s[:], in_=z_bf[:, t].rearrange("p m r -> p (m r)"))
            s_ps.append(psum.tile([P, N], F32, name=f"s{t}", tag=f"low{t}"))
            nc.tensor.matmul_mx(
                out=s_ps[t][:], lhsT=z_w[:].bitcast(FP8X4), lhsT_scale=z_s[:],
                rhs=z2_w[:].bitcast(FP8X4), rhs_scale=z2_s[:], start=True, stop=True,
            )
            ex.append(window(f"ex{t}"))
            nc.scalar.activation(ex[t][:, :N], s_ps[t][:], ACT.Exp, scale=0.0625)

        logs, s_neg = [], []
        for t in range(PACK):
            total = sb(f"total{t}", [P, N], F32)
            s_neg.append(window(f"s_neg{t}"))
            if t == 0:
                nc.vector.tensor_scalar(s_neg[t][:, :N], s_ps[t][:], -0.0625, None, ALU.mult)
            if t < FUSED_EX:
                ex_again = sb(f"ex_again{t}", [P, N], F32)
                nc.vector.tensor_copy(ex_again[:], ex[t][:, :N])
                nc.vector.tensor_tensor(total[:], ex[t][:].indirect(n5_t[:]), ex_again[:], ALU.add)
            else:
                ex_n5 = sb(f"ex_n5_{t}", [P, N], F32)
                nc.scalar.activation(ex_n5[:], ex[t][:].indirect(n5_t[:]), ACT.Copy)
                nc.vector.tensor_tensor(total[:], ex_n5[:], ex[t][:, :N], ALU.add)
            if 0 < t < NEG_ON_VECTOR:
                nc.vector.tensor_scalar(s_neg[t][:, :N], s_ps[t][:], -0.0625, None, ALU.mult)
            if t >= NEG_ON_VECTOR:
                nc.scalar.activation(s_neg[t][:, :N], s_ps[t][:], ACT.Copy, scale=-0.0625)
            logs.append(sb(f"log{t}", [P, N], F32))
            for where in ([slice(0, N)] if t < PACK - 1 else [cols(0), cols(1)]):
                nc.scalar.activation(logs[t][:, where], total[:, where], ACT.Ln)

        out_rows = out_0.rearrange("(p t) v -> p t v", t=PACK)
        out_words = out_1[0].rearrange("p n t -> p (n t)").bitcast(I32)
        y = sb("y", [P, PACK, N], F32)
        for t in range(PACK):
            if t < PACK - 1:
                nc.vector.tensor_tensor(y[:, t, :], s_neg[t][:].indirect(n6_t[:]), logs[t][:], ALU.add)
                nc.sync.dma_start(out_rows[:, t, :], y[:, t, :])
            else:
                for h in range(2):
                    nc.vector.tensor_tensor(y[:, t, cols(h)], s_neg[t][:].indirect(half_of(n6_t, h)), logs[t][:, cols(h)], ALU.add)
                    nc.sync.dma_start(out_rows[:, t, cols(h)], y[:, t, cols(h)])
        y_bf = [sb(f"y_bf{h}", [P, HALF, PACK], BF16) for h in range(2)]
        for h, copy in enumerate((nc.scalar.copy, nc.vector.tensor_copy)):
            copy(y_bf[h][:], y[:, :, cols(h)].rearrange("p t c -> p c t"))
        y_s = sb("y_s", [P, N], U8)
        for h in range(2):
            y_w = sb(f"y_w{h}", [P, HALF], U32)
            nc.vector.quantize_mx(out=y_w[:].bitcast(FP8X4), scales=y_s[:, cols(h)], in_=y_bf[h][:].rearrange("p c t -> p (c t)"))
            nc.sync.dma_start(out_words[:, cols(h)], y_w[:].bitcast(I32))
        scale_rows = out_2[0].bitcast(I32).rearrange("(q i) n -> i q n", i=4)
        for i in range(4):
            nc.scalar.dma_start(scale_rows[i], y_s[i:P:32, :].bitcast(I32))
